import numpy as np
import ml_dtypes


def mxq(x, axis, fmt="e4m3"):
    dtype, down = {"e4m3": (ml_dtypes.float8_e4m3fn, 7), "e5m2": (ml_dtypes.float8_e5m2, 14)}[fmt]
    v = np.moveaxis(np.asarray(x, np.float32).astype(ml_dtypes.bfloat16).astype(np.float64), axis, -1)
    blocks = v.reshape(v.shape[:-1] + (-1, 32))
    amax = np.abs(blocks).max(-1, keepdims=True)
    byte = np.maximum(np.where(amax > 0, np.frexp(amax)[1] - 1 + 127, 0) - down, 1)
    scale = np.exp2(byte - 127.0)
    codes = (blocks / scale).astype(np.float32).astype(dtype).astype(np.float64)
    return np.moveaxis((codes * scale).reshape(v.shape), -1, axis)


WIDE = False


def mx_kscale(k):
    if not WIDE:
        return np.ones(k)
    levels = np.array([10, -10, 5, -5, 0])
    if k % 512:
        return np.exp2(np.random.permutation(np.resize(levels, k // 32))).repeat(32)
    a = np.empty((k // 512, 16))
    for p in range(k // 512):
        a[p, :8] = np.random.permutation(np.resize(levels, 8))
        for g in range(8):
            far = levels[np.abs(levels - a[p, g]) >= 10]
            a[p, g + 8] = far[np.random.randint(len(far))]
    return np.exp2(a.ravel()).repeat(32)


def f64(x):
    return np.asarray(x).astype(np.float64)


def striped(idx):
    return np.tile(idx.reshape(-1, 16).T, (8, 1)).astype(np.uint16)


def unstriped(offs):
    return offs[:16].T.reshape(-1).astype(np.int64)


E2M1 = np.array([0.0, 0.5, 1.0, 1.5, 2.0, 3.0, 4.0, 6.0, -0.0, -0.5, -1.0, -1.5, -2.0, -3.0, -4.0, -6.0])


def pack_weight(w, fmt):
    k, n = w.shape
    w = f64(np.asarray(w, np.float32).astype(ml_dtypes.bfloat16)).reshape(k // 32, 32, n)
    amax = np.abs(w).max(1)
    if fmt == "e4m3":
        byte = np.frexp(amax)[1] - 1 + 127 - 7
    else:
        mant, ex = np.frexp(amax / 6.0)
        byte = np.where(mant > 0.5, ex, ex - 1) + 127
    byte = np.clip(np.where(amax > 0, byte, 1), 1, 254)
    scaled = (w * np.exp2(127.0 - byte)[:, None, :]).reshape(k, n).astype(np.float32)
    by_word = np.ascontiguousarray(scaled.reshape(k // 512, 128, 4, n).transpose(0, 1, 3, 2))
    if fmt == "e4m3":
        words = by_word.astype(ml_dtypes.float8_e4m3fn).view(np.uint8)
    else:
        c = by_word.astype(ml_dtypes.float4_e2m1fn).view(np.uint8) & 0xF
        words = (c[..., 0::2] | (c[..., 1::2] << 4)).reshape(k // 512, 128, 2 * n)
    return np.ascontiguousarray(words), np.ascontiguousarray(byte.astype(np.uint8).reshape(k // 512, 16, n))


def unpack_weight(words, scales, fmt):
    g, _, n = scales.shape
    words = np.ascontiguousarray(words).reshape(g, 128, n, -1)
    if fmt == "e4m3":
        vals = words.view(ml_dtypes.float8_e4m3fn).astype(np.float64)
    else:
        nib = np.empty((g, 128, n, 4), np.uint8)
        nib[..., 0::2] = words & 0xF
        nib[..., 1::2] = words >> 4
        vals = E2M1[nib]
    vals = vals * np.repeat(np.exp2(scales.astype(np.float64) - 127.0), 8, axis=1)[..., None]
    return vals.transpose(0, 1, 3, 2).reshape(g * 512, n)


def silu(v):
    return v / (1.0 + np.exp(-np.maximum(v, -700.0)))


def d_silu(v):
    s = 1.0 / (1.0 + np.exp(-np.maximum(v, -700.0)))
    return s * (1.0 + v * (1.0 - s))


K, T, E, C, H, N = 256, 768, 12, 256, 512, 512
TOP = 4


def by_expert(wq, xq):
    return np.concatenate([wq[e].T @ xq[:, e * C:(e + 1) * C] for e in range(E)], axis=1)


def setup_inputs():
    n = np.random.standard_normal
    s = mx_kscale(N)[:, None]
    u = mx_kscale(H)
    deal = np.repeat(np.arange(E), C).reshape(TOP, T)[:, np.random.permutation(T)]
    deal = np.take_along_axis(deal, np.argsort(np.random.rand(TOP, T), axis=0), axis=0)
    for _ in range(8):
        s_, t_ = np.random.permutation(T).reshape(2, -1); r = np.random.randint(TOP, size=T // 2); x, y = deal[r, s_].copy(), deal[r, t_].copy()
        ok = ~((deal[:, s_] == y).any(0) | (deal[:, t_] == x).any(0)); deal[r[ok], s_[ok]] = y[ok]; deal[r[ok], t_[ok]] = x[ok]
    order = np.lexsort((np.random.rand(TOP * T), deal.reshape(-1)))
    slot_token = order % T; pos = np.empty(TOP * T, np.int64); pos[order] = np.arange(TOP * T); pos = pos.reshape(TOP, T)
    g = np.random.uniform(0.5, 1.5, (TOP, T)); g = g / g.sum(0)
    w_slot = np.empty(E * C)
    for r in range(TOP): w_slot[pos[r]] = g[r]
    dy = pack_weight(n((N, T)) * s, "e4m3")
    w2 = [pack_weight(m, "e2m1") for m in n((E, N, H)) / np.sqrt(N) / s[None] * u[None, None, :]]
    w1 = [pack_weight(m, "e2m1") for m in n((E, H, K)) / np.sqrt(H) / u[None, :, None]]
    w3 = [pack_weight(m, "e2m1") for m in n((E, H, K)) / np.sqrt(H) / u[None, :, None]]
    return {
        "dy_words": dy[0],
        "dy_scales": dy[1],
        "a1": n((H, E * C)).astype(np.float32),
        "a3": n((H, E * C)).astype(np.float32),
        "w2_words": np.stack([m[0] for m in w2]),
        "w2_scales": np.stack([m[1] for m in w2]),
        "w1_words": np.stack([m[0] for m in w1]),
        "w1_scales": np.stack([m[1] for m in w1]),
        "w3_words": np.stack([m[0] for m in w3]),
        "w3_scales": np.stack([m[1] for m in w3]),
        "gate": np.tile(w_slot, (H, 1)).astype(np.float32),
        "offs": striped(slot_token),
        "pos1": striped(pos[0]),
        "pos2": striped(pos[1]),
        "pos3": striped(pos[2]),
        "pos4": striped(pos[3]),
    }


def reference(dy_words, dy_scales, a1, a3, w2_words, w2_scales, w1_words, w1_scales, w3_words, w3_scales, gate, offs, pos1, pos2, pos3, pos4):
    idx = unstriped(offs)
    w2 = np.stack([unpack_weight(w2_words[e], w2_scales[e], "e2m1") for e in range(E)])
    w1 = np.stack([unpack_weight(w1_words[e], w1_scales[e], "e2m1") for e in range(E)])
    w3 = np.stack([unpack_weight(w3_words[e], w3_scales[e], "e2m1") for e in range(E)])
    gq = unpack_weight(dy_words, dy_scales, "e4m3")[:, idx]
    dh = f64(gate) * by_expert(w2, gq)
    da1 = dh * f64(a3) * d_silu(f64(a1))
    da3 = dh * silu(f64(a1))
    dx = by_expert(w1, mxq(da1, 0, "e4m3")) + by_expert(w3, mxq(da3, 0, "e4m3"))
    return dx[:, unstriped(pos1)] + dx[:, unstriped(pos2)] + dx[:, unstriped(pos3)] + dx[:, unstriped(pos4)]

@@ -1,0 +1,245 @@
+from contextlib import ExitStack
+
+import concourse.mybir as mybir
+from concourse.masks import make_identity
+
+K, T, E, C, H, N = 256, 768, 12, 256, 512, 512
+S = E * C
+FLOPS = 2 * S * N * H + 2 * 2 * S * H * K
+BYTES = 128 * T * 4 + 16 * T + 2 * H * S * 4 + E * (128 * 2 * H + 16 * H) + 2 * E * (128 * 2 * K + 16 * K) + S * 4 + 128 * 2 * (S + 4 * T) // 16 + K * T * 4
+
+F32 = mybir.dt.float32
+BF16 = mybir.dt.bfloat16
+I32 = mybir.dt.int32
+U32 = mybir.dt.uint32
+U16 = mybir.dt.uint16
+U8 = mybir.dt.uint8
+FP8X4 = mybir.dt.float8_e4m3fn_x4
+FP4X4 = mybir.dt.float4_e2m1fn_x4
+ACT = mybir.ActivationFunctionType
+ALU = mybir.AluOpType
+
+P = 128
+PACK = 4
+GATHER = 512
+BLOCKS = S // P
+
+
+def load_scale_rows(nc, plane, scales):
+    for r in range(4):
+        nc.sync.dma_start(
+            out=plane[r:P:32, :, :].bitcast(I32),
+            in_=scales[:, r:16:4, :].rearrange("g q n -> q g n").bitcast(I32),
+        )
+
+
+def tile_moe_bdx_glu_silu_kernel(
+    tc, dy_words, dy_scales, a1, a3, w2_words, w2_scales, w1_words, w1_scales, w3_words, w3_scales,
+    gate, offs, pos1, pos2, pos3, pos4, out,
+):
+    nc = tc.nc
+    with ExitStack() as ctx:
+        keep = ctx.enter_context(tc.tile_pool(name="keep", bufs=1))
+        stream = ctx.enter_context(tc.tile_pool(name="stream", bufs=4))
+        work = ctx.enter_context(tc.tile_pool(name="work", bufs=3))
+        psum_first = ctx.enter_context(tc.psum_pool(name="psum_first", bufs=2))
+        psum_dh = ctx.enter_context(tc.psum_pool(name="psum_dh", bufs=4))
+        psum_dx = ctx.enter_context(tc.psum_pool(name="psum_dx", bufs=2))
+
+        dy_plane = keep.tile([P, 1, T], U8, align_bytes=64)
+        w2_plane = keep.tile([P, E, H], U8, align_bytes=64)
+        w1_plane = keep.tile([P, E, K], U8, align_bytes=64)
+        w3_plane = keep.tile([P, E, K], U8, align_bytes=64)
+        gate_rows = keep.tile([P, P], F32)
+        identity = keep.tile([P, P], F32)
+        nc.vector.memset(dy_plane[:].bitcast(I32), 0)
+        nc.vector.memset(w2_plane[:].bitcast(I32), 0)
+        nc.gpsimd.memset(gate_rows[:], 0.0)
+        make_identity(nc, identity[:])
+        nc.gpsimd.memset(w1_plane[:].bitcast(I32), 0)
+        nc.gpsimd.memset(w3_plane[:].bitcast(I32), 0)
+
+        slot_list = keep.tile([P, S // 16], U16)
+        nc.sync.dma_start(slot_list[:], offs)
+        dy_table = keep.tile([P, T], U32, align_bytes=64)
+        nc.sync.dma_start(out=dy_table[:].bitcast(I32), in_=dy_words[0].rearrange("p n t -> p (n t)").bitcast(I32))
+
+        def load_saved(src, e, name):
+            rows = stream.tile([P, PACK, C], F32, name=name)
+            nc.sync.dma_start(out=rows[:], in_=src[:, e * C:(e + 1) * C].rearrange("(p t) c -> p t c", t=PACK))
+            return rows
+
+        codes_of = {}
+
+        def load_words(src, first, last, width, name):
+            words = keep.tile([P, last - first, 2 * width], U8, name="%s_%d" % (name, first), align_bytes=64)
+            nc.sync.dma_start(out=words[:].bitcast(I32), in_=src[first:last, 0].rearrange("e p n -> p e n").bitcast(I32))
+            for e in range(first, last):
+                codes_of[name, e] = words[:, e - first, :]
+
+        a1_of, a3_of = {}, {}
+        a1_of[0] = load_saved(a1, 0, "a1_rows")
+        load_scale_rows(nc, dy_plane, dy_scales)
+        load_words(w2_words, 0, 2, H, "w2")
+        load_scale_rows(nc, w2_plane, w2_scales[:, 0])
+        a1_of[1] = load_saved(a1, 1, "a1_rows")
+        a3_of[0] = load_saved(a3, 0, "a3_rows")
+        a1_of[2] = load_saved(a1, 2, "a1_rows")
+        load_words(w2_words, 2, 6, H, "w2")
+        a3_of[1] = load_saved(a3, 1, "a3_rows")
+        load_scale_rows(nc, w1_plane, w1_scales[:, 0])
+        load_scale_rows(nc, w3_plane, w3_scales[:, 0])
+        load_words(w1_words, 0, 4, K, "w1")
+        load_words(w3_words, 0, 4, K, "w3")
+        nc.scalar.dma_start(out=gate_rows[0:BLOCKS, :], in_=gate[0].rearrange("(b q) -> b q", q=P))
+
+        gate_turned = psum_dx.tile([P, 2, C], F32, name="dx_sums")
+        nc.tensor.transpose(gate_turned[:, 0, 0:P], gate_rows[:], identity[:])
+        gate_cols = keep.tile([P, BLOCKS], F32)
+        nc.vector.tensor_copy(out=gate_cols[:], in_=gate_turned[:, 0, 0:BLOCKS])
+
+        g_words, g_scales = [], []
+
+        def gather_gradients(n):
+            entries = slot_list[:, n * GATHER // 16:(n + 1) * GATHER // 16]
+            words = keep.tile([P, GATHER], U32, name="g_words%d" % n, align_bytes=64)
+            scales = keep.tile([P, GATHER], U8, name="g_scales%d" % n, align_bytes=64)
+            nc.vector.tensor_copy(out=words[:], in_=dy_table[:].indirect(entries))
+            nc.vector.tensor_copy(out=scales[:], in_=dy_plane[:, 0, :].indirect(entries))
+            g_words.append(words)
+            g_scales.append(scales)
+
+        dx_rows = [keep.tile([P, S], F32, name="dx_rows%d" % kb) for kb in range(K // P)]
+        made = {}
+
+        def activations(e):
+            v = a1_of[e]
+            s = work.tile([P, PACK, C], F32, name="silu")
+            th = work.tile([P, PACK, C], F32, name="tanh_half")
+            q = work.tile([P, PACK, C], F32, name="one_minus_r")
+            nc.scalar.activation(out=s[:], in_=v[:], func=ACT.Silu)
+            nc.scalar.activation(out=th[:], in_=v[:], func=ACT.Tanh, scale=0.5)
+            nc.scalar.activation(out=q[:], in_=th[:], func=ACT.Copy, scale=-0.5, bias=0.5)
+            made[e] = [s, q]
+
+        def first_product(e):
+            w2_codes = codes_of["w2", e]
+            banks = []
+            for h in range(C // P):
+                b = e * (C // P) + h
+                n, c0 = divmod(b * P, GATHER)
+                sums = psum_first.tile([P, H], F32, name="first_sums")
+                nc.tensor.matmul_mx(
+                    out=sums[:],
+                    lhsT=g_words[n][:, c0:c0 + P].bitcast(FP8X4), lhsT_scale=g_scales[n][:, c0:c0 + P],
+                    rhs=w2_codes.bitcast(FP4X4), rhs_scale=w2_plane[:, e, :],
+                    start=True, stop=True,
+                )
+                dh_slots = work.tile([P, PACK, P], F32, name="dh_slots")
+                nc.scalar.activation(
+                    out=dh_slots[:], in_=sums[:].rearrange("s (m t) -> s t m", t=PACK),
+                    func=ACT.Copy, scale=gate_cols[:, b:b + 1],
+                )
+                dh = psum_dh.tile([P, PACK, P], F32, name="dh")
+                for t in range(PACK):
+                    nc.tensor.transpose(dh[:, t, :], dh_slots[:, t, :], identity[:])
+                banks.append(dh)
+            made[e] = made[e] + banks
+
+        def paired(ap):
+            return ap.rearrange("p t (c i) -> p c t i", i=2)
+
+        HALVES = C // P
+
+        def factors(e):
+            s, q = made[e][0:2]
+            w = work.tile([P, PACK, C], F32, name="d_minus_one")
+            f = work.tile([P, PACK, C], F32, name="a3_times_d")
+            nc.vector.scalar_tensor_tensor(out=w[:], in0=s[:], scalar=-1.0, in1=q[:], op0=ALU.add, op1=ALU.mult)
+            return w, f
+
+        def times_dh(e, da, h, j, factor):
+            nc.vector.tensor_tensor(
+                out=da[:, h, j].rearrange("p (c i) t -> p c t i", i=2),
+                in0=paired(made[e][2 + h][:]), in1=paired(factor[:, :, h * P:(h + 1) * P]), op=ALU.mult)
+
+        def quantise(da, codes, scales, h0, h1):
+            nc.vector.quantize_mx(
+                out=codes[:, h0:h1].rearrange("p h j c -> p (h j c)").bitcast(FP8X4),
+                scales=scales[:, h0:h1].rearrange("p h j c -> p (h j c)"),
+                in_=da[:, h0:h1].rearrange("p h j c t -> p (h j c t)"),
+            )
+
+        def second_product(e, codes, scales, h0, h1):
+            sums = psum_dx.tile([P, 2, C], F32, name="dx_sums")
+            for kb in range(K // P):
+                for h in range(h0, h1):
+                    for j, (name, plane) in enumerate((("w1", w1_plane), ("w3", w3_plane))):
+                        nc.tensor.matmul_mx(
+                            out=sums[:, kb, h * P:(h + 1) * P],
+                            lhsT=codes_of[name, e][:, 2 * kb * P:2 * (kb + 1) * P].bitcast(FP4X4),
+                            lhsT_scale=plane[:, e, kb * P:(kb + 1) * P],
+                            rhs=codes[:, h, j].bitcast(FP8X4), rhs_scale=scales[:, h, j],
+                            start=(j == 0), stop=(j == 1),
+                        )
+            for kb in range(K // P):
+                nc.scalar.copy(out=dx_rows[kb][:, e * C + h0 * P:e * C + h1 * P], in_=sums[:, kb, h0 * P:h1 * P])
+
+        def hidden_gradients(e):
+            s = made[e][0]
+            w, f = factors(e)
+            da = work.tile([P, HALVES, 2, P, PACK], BF16, name="da", align_bytes=64)
+            times_dh(e, da, 0, 1, s)
+            nc.vector.scalar_tensor_tensor(out=f[:], in0=w[:], scalar=1.0, in1=a3_of[e][:], op0=ALU.add, op1=ALU.mult)
+            times_dh(e, da, 1, 1, s)
+            times_dh(e, da, 0, 0, f)
+            times_dh(e, da, 1, 0, f)
+            made[e] = da
+
+        def finish(e):
+            codes = work.tile([P, HALVES, 2, P], U32, name="da_codes", align_bytes=64)
+            scales = work.tile([P, HALVES, 2, P], U8, name="da_scales", align_bytes=64)
+            pieces = [(0, HALVES)] if e < E - 1 else [(h, h + 1) for h in range(HALVES)]
+            for h0, h1 in pieces:
+                quantise(made[e], codes, scales, h0, h1)
+                second_product(e, codes, scales, h0, h1)
+
+        back_lists = []
+        for e in range(E + 2):
+            if e + 3 < E:
+                a1_of[e + 3] = load_saved(a1, e + 3, "a1_rows")
+            if e + 2 < E:
+                a3_of[e + 2] = load_saved(a3, e + 2, "a3_rows")
+            if e == 1:
+                load_words(w2_words, 6, E, H, "w2")
+                load_words(w1_words, 4, E, K, "w1")
+                load_words(w3_words, 4, E, K, "w3")
+            if e == 2:
+                for r, pos in enumerate((pos1, pos2, pos3, pos4)):
+                    entries = keep.tile([P, T // 16], U16, name="back_list%d" % r)
+                    nc.sync.dma_start(entries[:], pos)
+                    back_lists.append(entries)
+            if e < E:
+                if e * C % GATHER == 0:
+                    gather_gradients(e * C // GATHER)
+                activations(e)
+                first_product(e)
+            if 1 <= e <= E:
+                hidden_gradients(e - 1)
+            if 2 <= e:
+                finish(e - 2)
+
+        totals = [None] * (K // P)
+        for r in range(4):
+            for kb in range(K // P):
+                more = keep.tile([P, T], F32, name="total%d_%d" % (kb, r))
+                last = r == 3 and kb == K // P - 1
+                for c0, c1 in ([(0, 512), (512, T)] if last else [(0, T)]):
+                    picked = dx_rows[kb][:].indirect(back_lists[r][:, c0 // 16:c1 // 16])
+                    if r == 0:
+                        nc.vector.tensor_copy(out=more[:, c0:c1], in_=picked)
+                    else:
+                        nc.vector.tensor_tensor(out=more[:, c0:c1], in0=picked, in1=totals[kb][:, c0:c1], op=ALU.add)
+                    if r == 3:
+                        nc.sync.dma_start(out=out[kb * P:(kb + 1) * P, c0:c1], in_=more[:, c0:c1])
+                totals[kb] = more

@@ -23,6 +23,7 @@ P = 128
 PACK = 4
 GATHER = 512
 BLOCKS = S // P
+POOL_COLS = 640
 
 
 def load_scale_rows(nc, plane, scales):
@@ -42,18 +43,21 @@ def tile_moe_bdx_glu_silu_kernel(
         keep = ctx.enter_context(tc.tile_pool(name="keep", bufs=1))
         stream = ctx.enter_context(tc.tile_pool(name="stream", bufs=4))
         work = ctx.enter_context(tc.tile_pool(name="work", bufs=3))
+        single = ctx.enter_context(tc.tile_pool(name="single", bufs=1))
         psum_first = ctx.enter_context(tc.psum_pool(name="psum_first", bufs=2))
         psum_dh = ctx.enter_context(tc.psum_pool(name="psum_dh", bufs=4))
         psum_dx = ctx.enter_context(tc.psum_pool(name="psum_dx", bufs=2))
 
         dy_plane = keep.tile([P, 1, T], U8, align_bytes=64)
-        w2_plane = keep.tile([P, E, H], U8, align_bytes=64)
+        w2_plane_first = keep.tile([P, 2, H], U8, align_bytes=64)
+        w2_plane_rest = keep.tile([P, E - 2, H], U8, align_bytes=64)
         w1_plane = keep.tile([P, E, K], U8, align_bytes=64)
         w3_plane = keep.tile([P, E, K], U8, align_bytes=64)
         gate_rows = keep.tile([P, P], F32)
         identity = keep.tile([P, P], F32)
         nc.vector.memset(dy_plane[:].bitcast(I32), 0)
-        nc.vector.memset(w2_plane[:].bitcast(I32), 0)
+        nc.vector.memset(w2_plane_first[:].bitcast(I32), 0)
+        nc.vector.memset(w2_plane_rest[:].bitcast(I32), 0)
         nc.gpsimd.memset(gate_rows[:], 0.0)
         make_identity(nc, identity[:])
         nc.gpsimd.memset(w1_plane[:].bitcast(I32), 0)
@@ -61,6 +65,7 @@ def tile_moe_bdx_glu_silu_kernel(
 
         slot_list = keep.tile([P, S // 16], U16)
         nc.sync.dma_start(slot_list[:], offs)
+        load_scale_rows(nc, dy_plane, dy_scales)
         dy_table = keep.tile([P, T], U32, align_bytes=64)
         nc.sync.dma_start(out=dy_table[:].bitcast(I32), in_=dy_words[0].rearrange("p n t -> p (n t)").bitcast(I32))
 
@@ -79,19 +84,19 @@ def tile_moe_bdx_glu_silu_kernel(
 
         a1_of, a3_of = {}, {}
         a1_of[0] = load_saved(a1, 0, "a1_rows")
-        load_scale_rows(nc, dy_plane, dy_scales)
         load_words(w2_words, 0, 2, H, "w2")
-        load_scale_rows(nc, w2_plane, w2_scales[:, 0])
+        load_scale_rows(nc, w2_plane_first, w2_scales[0:2, 0])
+        nc.sync.dma_start(out=gate_rows[0:BLOCKS, :], in_=gate[0].rearrange("(b q) -> b q", q=P))
         a1_of[1] = load_saved(a1, 1, "a1_rows")
         a3_of[0] = load_saved(a3, 0, "a3_rows")
         a1_of[2] = load_saved(a1, 2, "a1_rows")
-        load_words(w2_words, 2, 6, H, "w2")
-        a3_of[1] = load_saved(a3, 1, "a3_rows")
         load_scale_rows(nc, w1_plane, w1_scales[:, 0])
         load_scale_rows(nc, w3_plane, w3_scales[:, 0])
+        load_scale_rows(nc, w2_plane_rest, w2_scales[2:E, 0])
+        a3_of[1] = load_saved(a3, 1, "a3_rows")
         load_words(w1_words, 0, 4, K, "w1")
         load_words(w3_words, 0, 4, K, "w3")
-        nc.scalar.dma_start(out=gate_rows[0:BLOCKS, :], in_=gate[0].rearrange("(b q) -> b q", q=P))
+        load_words(w2_words, 2, 6, H, "w2")
 
         gate_turned = psum_dx.tile([P, 2, C], F32, name="dx_sums")
         nc.tensor.transpose(gate_turned[:, 0, 0:P], gate_rows[:], identity[:])
@@ -102,8 +107,8 @@ def tile_moe_bdx_glu_silu_kernel(
 
         def gather_gradients(n):
             entries = slot_list[:, n * GATHER // 16:(n + 1) * GATHER // 16]
-            words = keep.tile([P, GATHER], U32, name="g_words%d" % n, align_bytes=64)
-            scales = keep.tile([P, GATHER], U8, name="g_scales%d" % n, align_bytes=64)
+            words = work.tile([P, GATHER], U32, name="g_words", align_bytes=64)
+            scales = work.tile([P, GATHER], U8, name="g_scales", align_bytes=64)
             nc.vector.tensor_copy(out=words[:], in_=dy_table[:].indirect(entries))
             nc.vector.tensor_copy(out=scales[:], in_=dy_plane[:, 0, :].indirect(entries))
             g_words.append(words)
@@ -112,15 +117,20 @@ def tile_moe_bdx_glu_silu_kernel(
         dx_rows = [keep.tile([P, S], F32, name="dx_rows%d" % kb) for kb in range(K // P)]
         made = {}
 
+        def flat(tile):
+            return tile[:].rearrange("p t c -> p (t c)")
+
         def activations(e):
             v = a1_of[e]
             s = work.tile([P, PACK, C], F32, name="silu")
-            th = work.tile([P, PACK, C], F32, name="tanh_half")
-            q = work.tile([P, PACK, C], F32, name="one_minus_r")
+            th = work.tile([P, PACK * C], F32, name="tanh_half")
+            s_less_one = work.tile([P, POOL_COLS], F32, name="s_less_one")
+            q = work.tile([P, PACK * C - POOL_COLS], F32, name="one_minus_r")
             nc.scalar.activation(out=s[:], in_=v[:], func=ACT.Silu)
-            nc.scalar.activation(out=th[:], in_=v[:], func=ACT.Tanh, scale=0.5)
-            nc.scalar.activation(out=q[:], in_=th[:], func=ACT.Copy, scale=-0.5, bias=0.5)
-            made[e] = [s, q]
+            nc.scalar.activation(out=th[:], in_=flat(v), func=ACT.Tanh, scale=0.5)
+            nc.scalar.activation(out=s_less_one[:], in_=flat(s)[:, 0:POOL_COLS], func=ACT.Copy, bias=-1.0)
+            nc.scalar.activation(out=q[:], in_=th[:, POOL_COLS:], func=ACT.Copy, scale=-0.5, bias=0.5)
+            made[e] = [s, th, s_less_one, q]
 
         def first_product(e):
             w2_codes = codes_of["w2", e]
@@ -132,7 +142,7 @@ def tile_moe_bdx_glu_silu_kernel(
                 nc.tensor.matmul_mx(
                     out=sums[:],
                     lhsT=g_words[n][:, c0:c0 + P].bitcast(FP8X4), lhsT_scale=g_scales[n][:, c0:c0 + P],
-                    rhs=w2_codes.bitcast(FP4X4), rhs_scale=w2_plane[:, e, :],
+                    rhs=w2_codes.bitcast(FP4X4), rhs_scale=w2_plane_first[:, e, :] if e < 2 else w2_plane_rest[:, e - 2, :],
                     start=True, stop=True,
                 )
                 dh_slots = work.tile([P, PACK, P], F32, name="dh_slots")
@@ -151,17 +161,23 @@ def tile_moe_bdx_glu_silu_kernel(
 
         HALVES = C // P
 
-        def factors(e):
-            s, q = made[e][0:2]
-            w = work.tile([P, PACK, C], F32, name="d_minus_one")
-            f = work.tile([P, PACK, C], F32, name="a3_times_d")
-            nc.vector.scalar_tensor_tensor(out=w[:], in0=s[:], scalar=-1.0, in1=q[:], op0=ALU.add, op1=ALU.mult)
-            return w, f
+        d_less_one = {}
+
+        def derivative_on_gpsimd(e):
+            s, th, s_less_one, q = made[e][0:4]
+            w = single.tile([P, PACK * C], F32, name="d_less_one")
+            nc.gpsimd.tensor_scalar(out=w[:, 0:POOL_COLS], in0=th[:, 0:POOL_COLS], scalar1=-0.5, scalar2=0.5, op0=ALU.mult, op1=ALU.add)
+            nc.gpsimd.tensor_tensor(out=w[:, 0:POOL_COLS], in0=w[:, 0:POOL_COLS], in1=s_less_one[:], op=ALU.mult)
+            d_less_one[e] = w
+
+        def derivative_on_vector(e):
+            s, th, s_less_one, q = made[e][0:4]
+            nc.vector.scalar_tensor_tensor(out=d_less_one[e][:, POOL_COLS:], in0=flat(s)[:, POOL_COLS:], scalar=-1.0, in1=q[:], op0=ALU.add, op1=ALU.mult)
 
         def times_dh(e, da, h, j, factor):
             nc.vector.tensor_tensor(
                 out=da[:, h, j].rearrange("p (c i) t -> p c t i", i=2),
-                in0=paired(made[e][2 + h][:]), in1=paired(factor[:, :, h * P:(h + 1) * P]), op=ALU.mult)
+                in0=paired(made[e][4 + h][:]), in1=paired(factor[:, :, h * P:(h + 1) * P]), op=ALU.mult)
 
         def quantise(da, codes, scales, h0, h1):
             nc.vector.quantize_mx(
@@ -185,23 +201,27 @@ def tile_moe_bdx_glu_silu_kernel(
             for kb in range(K // P):
                 nc.scalar.copy(out=dx_rows[kb][:, e * C + h0 * P:e * C + h1 * P], in_=sums[:, kb, h0 * P:h1 * P])
 
+        quantiser_input = {}
+
         def hidden_gradients(e):
             s = made[e][0]
-            w, f = factors(e)
+            f = work.tile([P, PACK, C], F32, name="a3_times_d")
             da = work.tile([P, HALVES, 2, P, PACK], BF16, name="da", align_bytes=64)
+            nc.vector.scalar_tensor_tensor(out=flat(f), in0=d_less_one[e][:], scalar=1.0, in1=flat(a3_of[e]), op0=ALU.add, op1=ALU.mult)
+            if e + 1 < E:
+                derivative_on_gpsimd(e + 1)
             times_dh(e, da, 0, 1, s)
-            nc.vector.scalar_tensor_tensor(out=f[:], in0=w[:], scalar=1.0, in1=a3_of[e][:], op0=ALU.add, op1=ALU.mult)
-            times_dh(e, da, 1, 1, s)
             times_dh(e, da, 0, 0, f)
+            times_dh(e, da, 1, 1, s)
             times_dh(e, da, 1, 0, f)
-            made[e] = da
+            quantiser_input[e] = da
 
         def finish(e):
             codes = work.tile([P, HALVES, 2, P], U32, name="da_codes", align_bytes=64)
             scales = work.tile([P, HALVES, 2, P], U8, name="da_scales", align_bytes=64)
             pieces = [(0, HALVES)] if e < E - 1 else [(h, h + 1) for h in range(HALVES)]
             for h0, h1 in pieces:
-                quantise(made[e], codes, scales, h0, h1)
+                quantise(quantiser_input[e], codes, scales, h0, h1)
                 second_product(e, codes, scales, h0, h1)
 
         back_lists = []
@@ -224,10 +244,14 @@ def tile_moe_bdx_glu_silu_kernel(
                     gather_gradients(e * C // GATHER)
                 activations(e)
                 first_product(e)
+            if e == 0:
+                derivative_on_gpsimd(0)
             if 1 <= e <= E:
-                hidden_gradients(e - 1)
+                derivative_on_vector(e - 1)
             if 2 <= e:
                 finish(e - 2)
+            if 1 <= e <= E:
+                hidden_gradients(e - 1)
 
         totals = [None] * (K // P)
         for r in range(4):

@@ -23,7 +23,7 @@ P = 128
 PACK = 4
 GATHER = 512
 BLOCKS = S // P
-POOL_COLS = 640
+POOL_COLS = 448
 
 
 def load_scale_rows(nc, plane, scales):
@@ -43,6 +43,7 @@ def tile_moe_bdx_glu_silu_kernel(
         keep = ctx.enter_context(tc.tile_pool(name="keep", bufs=1))
         stream = ctx.enter_context(tc.tile_pool(name="stream", bufs=4))
         work = ctx.enter_context(tc.tile_pool(name="work", bufs=3))
+        gathered = ctx.enter_context(tc.tile_pool(name="gathered", bufs=2))
         single = ctx.enter_context(tc.tile_pool(name="single", bufs=1))
         psum_first = ctx.enter_context(tc.psum_pool(name="psum_first", bufs=2))
         psum_dh = ctx.enter_context(tc.psum_pool(name="psum_dh", bufs=4))
@@ -66,8 +67,6 @@ def tile_moe_bdx_glu_silu_kernel(
         slot_list = keep.tile([P, S // 16], U16)
         nc.sync.dma_start(slot_list[:], offs)
         load_scale_rows(nc, dy_plane, dy_scales)
-        dy_table = keep.tile([P, T], U32, align_bytes=64)
-        nc.sync.dma_start(out=dy_table[:].bitcast(I32), in_=dy_words[0].rearrange("p n t -> p (n t)").bitcast(I32))
 
         def load_saved(src, e, name):
             rows = stream.tile([P, PACK, C], F32, name=name)
@@ -84,6 +83,8 @@ def tile_moe_bdx_glu_silu_kernel(
 
         a1_of, a3_of = {}, {}
         a1_of[0] = load_saved(a1, 0, "a1_rows")
+        dy_table = keep.tile([P, T], U32, align_bytes=64)
+        nc.sync.dma_start(out=dy_table[:].bitcast(I32), in_=dy_words[0].rearrange("p n t -> p (n t)").bitcast(I32))
         load_words(w2_words, 0, 2, H, "w2")
         load_scale_rows(nc, w2_plane_first, w2_scales[0:2, 0])
         nc.sync.dma_start(out=gate_rows[0:BLOCKS, :], in_=gate[0].rearrange("(b q) -> b q", q=P))
@@ -103,16 +104,17 @@ def tile_moe_bdx_glu_silu_kernel(
         gate_cols = keep.tile([P, BLOCKS], F32)
         nc.vector.tensor_copy(out=gate_cols[:], in_=gate_turned[:, 0, 0:BLOCKS])
 
-        g_words, g_scales = [], []
+        g_words, g_scales = {}, {}
 
-        def gather_gradients(n):
-            entries = slot_list[:, n * GATHER // 16:(n + 1) * GATHER // 16]
-            words = work.tile([P, GATHER], U32, name="g_words", align_bytes=64)
-            scales = work.tile([P, GATHER], U8, name="g_scales", align_bytes=64)
-            nc.vector.tensor_copy(out=words[:], in_=dy_table[:].indirect(entries))
-            nc.vector.tensor_copy(out=scales[:], in_=dy_plane[:, 0, :].indirect(entries))
-            g_words.append(words)
-            g_scales.append(scales)
+        def gather_scales(n):
+            scales = gathered.tile([P, GATHER], U8, name="g_scales", align_bytes=64)
+            nc.vector.tensor_copy(out=scales[:], in_=dy_plane[:, 0, :].indirect(slot_list[:, n * GATHER // 16:(n + 1) * GATHER // 16]))
+            g_scales[n] = scales
+
+        def gather_words(n):
+            words = gathered.tile([P, GATHER], U32, name="g_words", align_bytes=64)
+            nc.vector.tensor_copy(out=words[:], in_=dy_table[:].indirect(slot_list[:, n * GATHER // 16:(n + 1) * GATHER // 16]))
+            g_words[n] = words
 
         dx_rows = [keep.tile([P, S], F32, name="dx_rows%d" % kb) for kb in range(K // P)]
         made = {}
@@ -120,17 +122,21 @@ def tile_moe_bdx_glu_silu_kernel(
         def flat(tile):
             return tile[:].rearrange("p t c -> p (t c)")
 
+        def pool_cols(e):
+            return POOL_COLS if e > 0 else 0
+
         def activations(e):
             v = a1_of[e]
+            g = pool_cols(e)
             s = work.tile([P, PACK, C], F32, name="silu")
             th = work.tile([P, PACK * C], F32, name="tanh_half")
-            s_less_one = work.tile([P, POOL_COLS], F32, name="s_less_one")
-            q = work.tile([P, PACK * C - POOL_COLS], F32, name="one_minus_r")
+            shifted = work.tile([P, PACK * C], F32, name="shifted")
             nc.scalar.activation(out=s[:], in_=v[:], func=ACT.Silu)
             nc.scalar.activation(out=th[:], in_=flat(v), func=ACT.Tanh, scale=0.5)
-            nc.scalar.activation(out=s_less_one[:], in_=flat(s)[:, 0:POOL_COLS], func=ACT.Copy, bias=-1.0)
-            nc.scalar.activation(out=q[:], in_=th[:, POOL_COLS:], func=ACT.Copy, scale=-0.5, bias=0.5)
-            made[e] = [s, th, s_less_one, q]
+            if g:
+                nc.scalar.activation(out=shifted[:, 0:g], in_=flat(s)[:, 0:g], func=ACT.Copy, bias=-1.0)
+            nc.scalar.activation(out=shifted[:, g:], in_=th[:, g:], func=ACT.Copy, scale=-0.5, bias=0.5)
+            made[e] = [s, th, shifted]
 
         def first_product(e):
             w2_codes = codes_of["w2", e]
@@ -164,20 +170,23 @@ def tile_moe_bdx_glu_silu_kernel(
         d_less_one = {}
 
         def derivative_on_gpsimd(e):
-            s, th, s_less_one, q = made[e][0:4]
+            s, th, shifted = made[e][0:3]
+            g = pool_cols(e)
             w = single.tile([P, PACK * C], F32, name="d_less_one")
-            nc.gpsimd.tensor_scalar(out=w[:, 0:POOL_COLS], in0=th[:, 0:POOL_COLS], scalar1=-0.5, scalar2=0.5, op0=ALU.mult, op1=ALU.add)
-            nc.gpsimd.tensor_tensor(out=w[:, 0:POOL_COLS], in0=w[:, 0:POOL_COLS], in1=s_less_one[:], op=ALU.mult)
+            if g:
+                nc.gpsimd.tensor_scalar(out=w[:, 0:g], in0=th[:, 0:g], scalar1=-0.5, scalar2=0.5, op0=ALU.mult, op1=ALU.add)
+                nc.gpsimd.tensor_tensor(out=w[:, 0:g], in0=w[:, 0:g], in1=shifted[:, 0:g], op=ALU.mult)
             d_less_one[e] = w
 
         def derivative_on_vector(e):
-            s, th, s_less_one, q = made[e][0:4]
-            nc.vector.scalar_tensor_tensor(out=d_less_one[e][:, POOL_COLS:], in0=flat(s)[:, POOL_COLS:], scalar=-1.0, in1=q[:], op0=ALU.add, op1=ALU.mult)
+            s, th, shifted = made[e][0:3]
+            g = pool_cols(e)
+            nc.vector.scalar_tensor_tensor(out=d_less_one[e][:, g:], in0=flat(s)[:, g:], scalar=-1.0, in1=shifted[:, g:], op0=ALU.add, op1=ALU.mult)
 
         def times_dh(e, da, h, j, factor):
             nc.vector.tensor_tensor(
                 out=da[:, h, j].rearrange("p (c i) t -> p c t i", i=2),
-                in0=paired(made[e][4 + h][:]), in1=paired(factor[:, :, h * P:(h + 1) * P]), op=ALU.mult)
+                in0=paired(made[e][3 + h][:]), in1=paired(factor[:, :, h * P:(h + 1) * P]), op=ALU.mult)
 
         def quantise(da, codes, scales, h0, h1):
             nc.vector.quantize_mx(
@@ -203,29 +212,35 @@ def tile_moe_bdx_glu_silu_kernel(
 
         quantiser_input = {}
 
+        def finish(e, h0, h1):
+            codes = work.tile([P, HALVES, 2, P], U32, name="da_codes", align_bytes=64)
+            scales = work.tile([P, HALVES, 2, P], U8, name="da_scales", align_bytes=64)
+            quantise(quantiser_input[e], codes, scales, h0, h1)
+            second_product(e, codes, scales, h0, h1)
+
         def hidden_gradients(e):
             s = made[e][0]
             f = work.tile([P, PACK, C], F32, name="a3_times_d")
             da = work.tile([P, HALVES, 2, P, PACK], BF16, name="da", align_bytes=64)
+            quantiser_input[e] = da
             nc.vector.scalar_tensor_tensor(out=flat(f), in0=d_less_one[e][:], scalar=1.0, in1=flat(a3_of[e]), op0=ALU.add, op1=ALU.mult)
             if e + 1 < E:
                 derivative_on_gpsimd(e + 1)
             times_dh(e, da, 0, 1, s)
             times_dh(e, da, 0, 0, f)
             times_dh(e, da, 1, 1, s)
+            if e == E - 1:
+                finish(e, 0, 1)
             times_dh(e, da, 1, 0, f)
-            quantiser_input[e] = da
-
-        def finish(e):
-            codes = work.tile([P, HALVES, 2, P], U32, name="da_codes", align_bytes=64)
-            scales = work.tile([P, HALVES, 2, P], U8, name="da_scales", align_bytes=64)
-            pieces = [(0, HALVES)] if e < E - 1 else [(h, h + 1) for h in range(HALVES)]
-            for h0, h1 in pieces:
-                quantise(quantiser_input[e], codes, scales, h0, h1)
-                second_product(e, codes, scales, h0, h1)
+            if e == E - 1:
+                finish(e, 1, 2)
 
         back_lists = []
-        for e in range(E + 2):
+        gather_scales(0)
+        gather_words(0)
+        gather_scales(1)
+        gather_words(1)
+        for e in range(E + 1):
             if e + 3 < E:
                 a1_of[e + 3] = load_saved(a1, e + 3, "a1_rows")
             if e + 2 < E:
@@ -240,8 +255,8 @@ def tile_moe_bdx_glu_silu_kernel(
                     nc.sync.dma_start(entries[:], pos)
                     back_lists.append(entries)
             if e < E:
-                if e * C % GATHER == 0:
-                    gather_gradients(e * C // GATHER)
+                if 2 <= e < E - 2:
+                    (gather_words if e % 2 else gather_scales)(e // 2 + 1)
                 activations(e)
                 first_product(e)
             if e == 0:
@@ -249,7 +264,7 @@ def tile_moe_bdx_glu_silu_kernel(
             if 1 <= e <= E:
                 derivative_on_vector(e - 1)
             if 2 <= e:
-                finish(e - 2)
+                finish(e - 2, 0, HALVES)
             if 1 <= e <= E:
                 hidden_gradients(e - 1)
 
@@ -258,7 +273,7 @@ def tile_moe_bdx_glu_silu_kernel(
             for kb in range(K // P):
                 more = keep.tile([P, T], F32, name="total%d_%d" % (kb, r))
                 last = r == 3 and kb == K // P - 1
-                for c0, c1 in ([(0, 512), (512, T)] if last else [(0, T)]):
+                for c0, c1 in ([(0, 576), (576, T)] if last else [(0, T)]):
                     picked = dx_rows[kb][:].indirect(back_lists[r][:, c0 // 16:c1 // 16])
                     if r == 0:
                         nc.vector.tensor_copy(out=more[:, c0:c1], in_=picked)

@@ -23,7 +23,7 @@ P = 128
 PACK = 4
 GATHER = 512
 BLOCKS = S // P
-POOL_COLS = 448
+POOL_COLS = 480
 
 
 def load_scale_rows(nc, plane, scales):
@@ -64,9 +64,6 @@ def tile_moe_bdx_glu_silu_kernel(
         nc.gpsimd.memset(w1_plane[:].bitcast(I32), 0)
         nc.gpsimd.memset(w3_plane[:].bitcast(I32), 0)
 
-        slot_list = keep.tile([P, S // 16], U16)
-        nc.sync.dma_start(slot_list[:], offs)
-        load_scale_rows(nc, dy_plane, dy_scales)
 
         def load_saved(src, e, name):
             rows = stream.tile([P, PACK, C], F32, name=name)
@@ -83,38 +80,44 @@ def tile_moe_bdx_glu_silu_kernel(
 
         a1_of, a3_of = {}, {}
         a1_of[0] = load_saved(a1, 0, "a1_rows")
+        slot_list = keep.tile([P, S // 16], U16)
+        nc.sync.dma_start(slot_list[:], offs)
+        load_scale_rows(nc, dy_plane, dy_scales)
         dy_table = keep.tile([P, T], U32, align_bytes=64)
         nc.sync.dma_start(out=dy_table[:].bitcast(I32), in_=dy_words[0].rearrange("p n t -> p (n t)").bitcast(I32))
         load_words(w2_words, 0, 2, H, "w2")
-        load_scale_rows(nc, w2_plane_first, w2_scales[0:2, 0])
         nc.sync.dma_start(out=gate_rows[0:BLOCKS, :], in_=gate[0].rearrange("(b q) -> b q", q=P))
-        a1_of[1] = load_saved(a1, 1, "a1_rows")
+        load_scale_rows(nc, w2_plane_first, w2_scales[0:2, 0])
         a3_of[0] = load_saved(a3, 0, "a3_rows")
+        a1_of[1] = load_saved(a1, 1, "a1_rows")
         a1_of[2] = load_saved(a1, 2, "a1_rows")
         load_scale_rows(nc, w1_plane, w1_scales[:, 0])
         load_scale_rows(nc, w3_plane, w3_scales[:, 0])
         load_scale_rows(nc, w2_plane_rest, w2_scales[2:E, 0])
+        load_words(w1_words, 0, 2, K, "w1")
+        load_words(w3_words, 0, 2, K, "w3")
+        load_words(w2_words, 2, 4, H, "w2")
         a3_of[1] = load_saved(a3, 1, "a3_rows")
-        load_words(w1_words, 0, 4, K, "w1")
-        load_words(w3_words, 0, 4, K, "w3")
-        load_words(w2_words, 2, 6, H, "w2")
 
         gate_turned = psum_dx.tile([P, 2, C], F32, name="dx_sums")
         nc.tensor.transpose(gate_turned[:, 0, 0:P], gate_rows[:], identity[:])
         gate_cols = keep.tile([P, BLOCKS], F32)
-        nc.vector.tensor_copy(out=gate_cols[:], in_=gate_turned[:, 0, 0:BLOCKS])
+        nc.scalar.copy(out=gate_cols[:], in_=gate_turned[:, 0, 0:BLOCKS])
 
         g_words, g_scales = {}, {}
 
+        def gather(table, dtype, name, found, n):
+            first, last = max(2 * n - 1, 0), min(2 * n + 1, E)
+            tile = gathered.tile([P, (last - first) * C], dtype, name=name, align_bytes=64)
+            nc.vector.tensor_copy(out=tile[:], in_=table.indirect(slot_list[:, first * C // 16:last * C // 16]))
+            for e in range(first, last):
+                found[e] = tile[:, (e - first) * C:(e - first + 1) * C]
+
         def gather_scales(n):
-            scales = gathered.tile([P, GATHER], U8, name="g_scales", align_bytes=64)
-            nc.vector.tensor_copy(out=scales[:], in_=dy_plane[:, 0, :].indirect(slot_list[:, n * GATHER // 16:(n + 1) * GATHER // 16]))
-            g_scales[n] = scales
+            gather(dy_plane[:, 0, :], U8, "g_scales", g_scales, n)
 
         def gather_words(n):
-            words = gathered.tile([P, GATHER], U32, name="g_words", align_bytes=64)
-            nc.vector.tensor_copy(out=words[:], in_=dy_table[:].indirect(slot_list[:, n * GATHER // 16:(n + 1) * GATHER // 16]))
-            g_words[n] = words
+            gather(dy_table[:], U32, "g_words", g_words, n)
 
         dx_rows = [keep.tile([P, S], F32, name="dx_rows%d" % kb) for kb in range(K // P)]
         made = {}
@@ -143,17 +146,17 @@ def tile_moe_bdx_glu_silu_kernel(
             banks = []
             for h in range(C // P):
                 b = e * (C // P) + h
-                n, c0 = divmod(b * P, GATHER)
                 sums = psum_first.tile([P, H], F32, name="first_sums")
                 nc.tensor.matmul_mx(
                     out=sums[:],
-                    lhsT=g_words[n][:, c0:c0 + P].bitcast(FP8X4), lhsT_scale=g_scales[n][:, c0:c0 + P],
+                    lhsT=g_words[e][:, h * P:(h + 1) * P].bitcast(FP8X4), lhsT_scale=g_scales[e][:, h * P:(h + 1) * P],
                     rhs=w2_codes.bitcast(FP4X4), rhs_scale=w2_plane_first[:, e, :] if e < 2 else w2_plane_rest[:, e - 2, :],
                     start=True, stop=True,
                 )
                 dh_slots = work.tile([P, PACK, P], F32, name="dh_slots")
                 nc.scalar.activation(
-                    out=dh_slots[:], in_=sums[:].rearrange("s (m t) -> s t m", t=PACK),
+                    out=dh_slots[:].rearrange("s t (c i) -> s c t i", i=4),
+                    in_=sums[:].rearrange("s (c i t) -> s c t i", i=4, t=PACK),
                     func=ACT.Copy, scale=gate_cols[:, b:b + 1],
                 )
                 dh = psum_dh.tile([P, PACK, P], F32, name="dh")
@@ -196,19 +199,24 @@ def tile_moe_bdx_glu_silu_kernel(
             )
 
         def second_product(e, codes, scales, h0, h1):
-            sums = psum_dx.tile([P, 2, C], F32, name="dx_sums")
+            if e == E - 1 and h1 == HALVES:
+                banks = [psum_first.tile([P, H], F32, name="first_sums") for kb in range(K // P)]
+                sums = [bank[:, 0:C] for bank in banks]
+            else:
+                bank = psum_dx.tile([P, 2, C], F32, name="dx_sums")
+                sums = [bank[:, kb, :] for kb in range(K // P)]
             for kb in range(K // P):
                 for h in range(h0, h1):
                     for j, (name, plane) in enumerate((("w1", w1_plane), ("w3", w3_plane))):
                         nc.tensor.matmul_mx(
-                            out=sums[:, kb, h * P:(h + 1) * P],
+                            out=sums[kb][:, h * P:(h + 1) * P],
                             lhsT=codes_of[name, e][:, 2 * kb * P:2 * (kb + 1) * P].bitcast(FP4X4),
                             lhsT_scale=plane[:, e, kb * P:(kb + 1) * P],
                             rhs=codes[:, h, j].bitcast(FP8X4), rhs_scale=scales[:, h, j],
                             start=(j == 0), stop=(j == 1),
                         )
             for kb in range(K // P):
-                nc.scalar.copy(out=dx_rows[kb][:, e * C + h0 * P:e * C + h1 * P], in_=sums[:, kb, h0 * P:h1 * P])
+                nc.scalar.copy(out=dx_rows[kb][:, e * C + h0 * P:e * C + h1 * P], in_=sums[kb][:, h0 * P:h1 * P])
 
         quantiser_input = {}
 
@@ -245,18 +253,22 @@ def tile_moe_bdx_glu_silu_kernel(
                 a1_of[e + 3] = load_saved(a1, e + 3, "a1_rows")
             if e + 2 < E:
                 a3_of[e + 2] = load_saved(a3, e + 2, "a3_rows")
+            if e == 0:
+                load_words(w1_words, 2, 6, K, "w1")
+                load_words(w3_words, 2, 6, K, "w3")
+                load_words(w2_words, 4, 8, H, "w2")
             if e == 1:
-                load_words(w2_words, 6, E, H, "w2")
-                load_words(w1_words, 4, E, K, "w1")
-                load_words(w3_words, 4, E, K, "w3")
+                load_words(w2_words, 8, E, H, "w2")
+                load_words(w1_words, 6, E, K, "w1")
+                load_words(w3_words, 6, E, K, "w3")
             if e == 2:
                 for r, pos in enumerate((pos1, pos2, pos3, pos4)):
                     entries = keep.tile([P, T // 16], U16, name="back_list%d" % r)
                     nc.sync.dma_start(entries[:], pos)
                     back_lists.append(entries)
             if e < E:
-                if 2 <= e < E - 2:
-                    (gather_words if e % 2 else gather_scales)(e // 2 + 1)
+                if 1 <= e < E - 1:
+                    (gather_scales if e % 2 else gather_words)((e + 3) // 2)
                 activations(e)
                 first_product(e)
             if e == 0:
@@ -273,7 +285,7 @@ def tile_moe_bdx_glu_silu_kernel(
             for kb in range(K // P):
                 more = keep.tile([P, T], F32, name="total%d_%d" % (kb, r))
                 last = r == 3 and kb == K // P - 1
-                for c0, c1 in ([(0, 576), (576, T)] if last else [(0, T)]):
+                for c0, c1 in ([(0, 640), (640, T)] if last else [(0, T)]):
                     picked = dx_rows[kb][:].indirect(back_lists[r][:, c0 // 16:c1 // 16])
                     if r == 0:
                         nc.vector.tensor_copy(out=more[:, c0:c1], in_=picked)

from contextlib import ExitStack

import concourse.mybir as mybir
from concourse.masks import make_identity

K, T, E, C, H, N = 256, 768, 12, 256, 512, 512
S = E * C
FLOPS = 2 * S * N * H + 2 * 2 * S * H * K
BYTES = 128 * T * 4 + 16 * T + 2 * H * S * 4 + E * (128 * 2 * H + 16 * H) + 2 * E * (128 * 2 * K + 16 * K) + S * 4 + 128 * 2 * (S + 4 * T) // 16 + K * T * 4

F32 = mybir.dt.float32
BF16 = mybir.dt.bfloat16
I32 = mybir.dt.int32
U32 = mybir.dt.uint32
U16 = mybir.dt.uint16
U8 = mybir.dt.uint8
FP8X4 = mybir.dt.float8_e4m3fn_x4
FP4X4 = mybir.dt.float4_e2m1fn_x4
ACT = mybir.ActivationFunctionType
ALU = mybir.AluOpType

P = 128
PACK = 4
GATHER = 512
BLOCKS = S // P
POOL_COLS = 480


def load_scale_rows(nc, plane, scales):
    for r in range(4):
        nc.sync.dma_start(
            out=plane[r:P:32, :, :].bitcast(I32),
            in_=scales[:, r:16:4, :].rearrange("g q n -> q g n").bitcast(I32),
        )


def tile_moe_bdx_glu_silu_kernel(
    tc, dy_words, dy_scales, a1, a3, w2_words, w2_scales, w1_words, w1_scales, w3_words, w3_scales,
    gate, offs, pos1, pos2, pos3, pos4, out,
):
    nc = tc.nc
    with ExitStack() as ctx:
        keep = ctx.enter_context(tc.tile_pool(name="keep", bufs=1))
        stream = ctx.enter_context(tc.tile_pool(name="stream", bufs=4))
        work = ctx.enter_context(tc.tile_pool(name="work", bufs=3))
        gathered = ctx.enter_context(tc.tile_pool(name="gathered", bufs=2))
        single = ctx.enter_context(tc.tile_pool(name="single", bufs=1))
        psum_first = ctx.enter_context(tc.psum_pool(name="psum_first", bufs=2))
        psum_dh = ctx.enter_context(tc.psum_pool(name="psum_dh", bufs=4))
        psum_dx = ctx.enter_context(tc.psum_pool(name="psum_dx", bufs=2))

        dy_plane = keep.tile([P, 1, T], U8, align_bytes=64)
        w2_plane_first = keep.tile([P, 2, H], U8, align_bytes=64)
        w2_plane_rest = keep.tile([P, E - 2, H], U8, align_bytes=64)
        w1_plane = keep.tile([P, E, K], U8, align_bytes=64)
        w3_plane = keep.tile([P, E, K], U8, align_bytes=64)
        gate_rows = keep.tile([P, P], F32)
        identity = keep.tile([P, P], F32)
        nc.vector.memset(dy_plane[:].bitcast(I32), 0)
        nc.vector.memset(w2_plane_first[:].bitcast(I32), 0)
        nc.vector.memset(w2_plane_rest[:].bitcast(I32), 0)
        nc.gpsimd.memset(gate_rows[:], 0.0)
        make_identity(nc, identity[:])
        nc.gpsimd.memset(w1_plane[:].bitcast(I32), 0)
        nc.gpsimd.memset(w3_plane[:].bitcast(I32), 0)


        def load_saved(src, e, name):
            rows = stream.tile([P, PACK, C], F32, name=name)
            nc.sync.dma_start(out=rows[:], in_=src[:, e * C:(e + 1) * C].rearrange("(p t) c -> p t c", t=PACK))
            return rows

        codes_of = {}

        def load_words(src, first, last, width, name):
            words = keep.tile([P, last - first, 2 * width], U8, name="%s_%d" % (name, first), align_bytes=64)
            nc.sync.dma_start(out=words[:].bitcast(I32), in_=src[first:last, 0].rearrange("e p n -> p e n").bitcast(I32))
            for e in range(first, last):
                codes_of[name, e] = words[:, e - first, :]

        a1_of, a3_of = {}, {}
        a1_of[0] = load_saved(a1, 0, "a1_rows")
        slot_list = keep.tile([P, S // 16], U16)
        nc.sync.dma_start(slot_list[:], offs)
        load_scale_rows(nc, dy_plane, dy_scales)
        dy_table = keep.tile([P, T], U32, align_bytes=64)
        nc.sync.dma_start(out=dy_table[:].bitcast(I32), in_=dy_words[0].rearrange("p n t -> p (n t)").bitcast(I32))
        load_words(w2_words, 0, 2, H, "w2")
        nc.sync.dma_start(out=gate_rows[0:BLOCKS, :], in_=gate[0].rearrange("(b q) -> b q", q=P))
        load_scale_rows(nc, w2_plane_first, w2_scales[0:2, 0])
        a3_of[0] = load_saved(a3, 0, "a3_rows")
        a1_of[1] = load_saved(a1, 1, "a1_rows")
        a1_of[2] = load_saved(a1, 2, "a1_rows")
        load_scale_rows(nc, w1_plane, w1_scales[:, 0])
        load_scale_rows(nc, w3_plane, w3_scales[:, 0])
        load_scale_rows(nc, w2_plane_rest, w2_scales[2:E, 0])
        load_words(w1_words, 0, 2, K, "w1")
        load_words(w3_words, 0, 2, K, "w3")
        load_words(w2_words, 2, 4, H, "w2")
        a3_of[1] = load_saved(a3, 1, "a3_rows")

        gate_turned = psum_dx.tile([P, 2, C], F32, name="dx_sums")
        nc.tensor.transpose(gate_turned[:, 0, 0:P], gate_rows[:], identity[:])
        gate_cols = keep.tile([P, BLOCKS], F32)
        nc.scalar.copy(out=gate_cols[:], in_=gate_turned[:, 0, 0:BLOCKS])

        g_words, g_scales = {}, {}

        def gather(table, dtype, name, found, n):
            first, last = max(2 * n - 1, 0), min(2 * n + 1, E)
            tile = gathered.tile([P, (last - first) * C], dtype, name=name, align_bytes=64)
            nc.vector.tensor_copy(out=tile[:], in_=table.indirect(slot_list[:, first * C // 16:last * C // 16]))
            for e in range(first, last):
                found[e] = tile[:, (e - first) * C:(e - first + 1) * C]

        def gather_scales(n):
            gather(dy_plane[:, 0, :], U8, "g_scales", g_scales, n)

        def gather_words(n):
            gather(dy_table[:], U32, "g_words", g_words, n)

        dx_rows = [keep.tile([P, S], F32, name="dx_rows%d" % kb) for kb in range(K // P)]
        made = {}

        def flat(tile):
            return tile[:].rearrange("p t c -> p (t c)")

        def pool_cols(e):
            return POOL_COLS if e > 0 else 0

        def activations(e):
            v = a1_of[e]
            g = pool_cols(e)
            s = work.tile([P, PACK, C], F32, name="silu")
            th = work.tile([P, PACK * C], F32, name="tanh_half")
            shifted = work.tile([P, PACK * C], F32, name="shifted")
            nc.scalar.activation(out=s[:], in_=v[:], func=ACT.Silu)
            nc.scalar.activation(out=th[:], in_=flat(v), func=ACT.Tanh, scale=0.5)
            if g:
                nc.scalar.activation(out=shifted[:, 0:g], in_=flat(s)[:, 0:g], func=ACT.Copy, bias=-1.0)
            nc.scalar.activation(out=shifted[:, g:], in_=th[:, g:], func=ACT.Copy, scale=-0.5, bias=0.5)
            made[e] = [s, th, shifted]

        def first_product(e):
            w2_codes = codes_of["w2", e]
            banks = []
            for h in range(C // P):
                b = e * (C // P) + h
                sums = psum_first.tile([P, H], F32, name="first_sums")
                nc.tensor.matmul_mx(
                    out=sums[:],
                    lhsT=g_words[e][:, h * P:(h + 1) * P].bitcast(FP8X4), lhsT_scale=g_scales[e][:, h * P:(h + 1) * P],
                    rhs=w2_codes.bitcast(FP4X4), rhs_scale=w2_plane_first[:, e, :] if e < 2 else w2_plane_rest[:, e - 2, :],
                    start=True, stop=True,
                )
                dh_slots = work.tile([P, PACK, P], F32, name="dh_slots")
                nc.scalar.activation(
                    out=dh_slots[:].rearrange("s t (c i) -> s c t i", i=4),
                    in_=sums[:].rearrange("s (c i t) -> s c t i", i=4, t=PACK),
                    func=ACT.Copy, scale=gate_cols[:, b:b + 1],
                )
                dh = psum_dh.tile([P, PACK, P], F32, name="dh")
                for t in range(PACK):
                    nc.tensor.transpose(dh[:, t, :], dh_slots[:, t, :], identity[:])
                banks.append(dh)
            made[e] = made[e] + banks

        def paired(ap):
            return ap.rearrange("p t (c i) -> p c t i", i=2)

        HALVES = C // P

        d_less_one = {}

        def derivative_on_gpsimd(e):
            s, th, shifted = made[e][0:3]
            g = pool_cols(e)
            w = single.tile([P, PACK * C], F32, name="d_less_one")
            if g:
                nc.gpsimd.tensor_scalar(out=w[:, 0:g], in0=th[:, 0:g], scalar1=-0.5, scalar2=0.5, op0=ALU.mult, op1=ALU.add)
                nc.gpsimd.tensor_tensor(out=w[:, 0:g], in0=w[:, 0:g], in1=shifted[:, 0:g], op=ALU.mult)
            d_less_one[e] = w

        def derivative_on_vector(e):
            s, th, shifted = made[e][0:3]
            g = pool_cols(e)
            nc.vector.scalar_tensor_tensor(out=d_less_one[e][:, g:], in0=flat(s)[:, g:], scalar=-1.0, in1=shifted[:, g:], op0=ALU.add, op1=ALU.mult)

        def times_dh(e, da, h, j, factor):
            nc.vector.tensor_tensor(
                out=da[:, h, j].rearrange("p (c i) t -> p c t i", i=2),
                in0=paired(made[e][3 + h][:]), in1=paired(factor[:, :, h * P:(h + 1) * P]), op=ALU.mult)

        def quantise(da, codes, scales, h0, h1):
            nc.vector.quantize_mx(
                out=codes[:, h0:h1].rearrange("p h j c -> p (h j c)").bitcast(FP8X4),
                scales=scales[:, h0:h1].rearrange("p h j c -> p (h j c)"),
                in_=da[:, h0:h1].rearrange("p h j c t -> p (h j c t)"),
            )

        def second_product(e, codes, scales, h0, h1):
            if e == E - 1 and h1 == HALVES:
                banks = [psum_first.tile([P, H], F32, name="first_sums") for kb in range(K // P)]
                sums = [bank[:, 0:C] for bank in banks]
            else:
                bank = psum_dx.tile([P, 2, C], F32, name="dx_sums")
                sums = [bank[:, kb, :] for kb in range(K // P)]
            for kb in range(K // P):
                for h in range(h0, h1):
                    for j, (name, plane) in enumerate((("w1", w1_plane), ("w3", w3_plane))):
                        nc.tensor.matmul_mx(
                            out=sums[kb][:, h * P:(h + 1) * P],
                            lhsT=codes_of[name, e][:, 2 * kb * P:2 * (kb + 1) * P].bitcast(FP4X4),
                            lhsT_scale=plane[:, e, kb * P:(kb + 1) * P],
                            rhs=codes[:, h, j].bitcast(FP8X4), rhs_scale=scales[:, h, j],
                            start=(j == 0), stop=(j == 1),
                        )
            for kb in range(K // P):
                nc.scalar.copy(out=dx_rows[kb][:, e * C + h0 * P:e * C + h1 * P], in_=sums[kb][:, h0 * P:h1 * P])

        quantiser_input = {}

        def finish(e, h0, h1):
            codes = work.tile([P, HALVES, 2, P], U32, name="da_codes", align_bytes=64)
            scales = work.tile([P, HALVES, 2, P], U8, name="da_scales", align_bytes=64)
            quantise(quantiser_input[e], codes, scales, h0, h1)
            second_product(e, codes, scales, h0, h1)

        def hidden_gradients(e):
            s = made[e][0]
            f = work.tile([P, PACK, C], F32, name="a3_times_d")
            da = work.tile([P, HALVES, 2, P, PACK], BF16, name="da", align_bytes=64)
            quantiser_input[e] = da
            nc.vector.scalar_tensor_tensor(out=flat(f), in0=d_less_one[e][:], scalar=1.0, in1=flat(a3_of[e]), op0=ALU.add, op1=ALU.mult)
            if e + 1 < E:
                derivative_on_gpsimd(e + 1)
            times_dh(e, da, 0, 1, s)
            times_dh(e, da, 0, 0, f)
            times_dh(e, da, 1, 1, s)
            if e == E - 1:
                finish(e, 0, 1)
            times_dh(e, da, 1, 0, f)
            if e == E - 1:
                finish(e, 1, 2)

        back_lists = []
        gather_scales(0)
        gather_words(0)
        gather_scales(1)
        gather_words(1)
        for e in range(E + 1):
            if e + 3 < E:
                a1_of[e + 3] = load_saved(a1, e + 3, "a1_rows")
            if e + 2 < E:
                a3_of[e + 2] = load_saved(a3, e + 2, "a3_rows")
            if e == 0:
                load_words(w1_words, 2, 6, K, "w1")
                load_words(w3_words, 2, 6, K, "w3")
                load_words(w2_words, 4, 8, H, "w2")
            if e == 1:
                load_words(w2_words, 8, E, H, "w2")
                load_words(w1_words, 6, E, K, "w1")
                load_words(w3_words, 6, E, K, "w3")
            if e == 2:
                for r, pos in enumerate((pos1, pos2, pos3, pos4)):
                    entries = keep.tile([P, T // 16], U16, name="back_list%d" % r)
                    nc.sync.dma_start(entries[:], pos)
                    back_lists.append(entries)
            if e < E:
                if 1 <= e < E - 1:
                    (gather_scales if e % 2 else gather_words)((e + 3) // 2)
                activations(e)
                first_product(e)
            if e == 0:
                derivative_on_gpsimd(0)
            if 1 <= e <= E:
                derivative_on_vector(e - 1)
            if 2 <= e:
                finish(e - 2, 0, HALVES)
            if 1 <= e <= E:
                hidden_gradients(e - 1)

        totals = [None] * (K // P)
        for r in range(4):
            for kb in range(K // P):
                more = keep.tile([P, T], F32, name="total%d_%d" % (kb, r))
                last = r == 3 and kb == K // P - 1
                for c0, c1 in ([(0, 640), (640, T)] if last else [(0, T)]):
                    picked = dx_rows[kb][:].indirect(back_lists[r][:, c0 // 16:c1 // 16])
                    if r == 0:
                        nc.vector.tensor_copy(out=more[:, c0:c1], in_=picked)
                    else:
                        nc.vector.tensor_tensor(out=more[:, c0:c1], in0=picked, in1=totals[kb][:, c0:c1], op=ALU.add)
                    if r == 3:
                        nc.sync.dma_start(out=out[kb * P:(kb + 1) * P, c0:c1], in_=more[:, c0:c1])
                totals[kb] = more
